import numpy as np
import ml_dtypes


def mxq(x, axis, fmt="e4m3"):
    dtype, down = {"e4m3": (ml_dtypes.float8_e4m3fn, 7), "e5m2": (ml_dtypes.float8_e5m2, 14)}[fmt]
    v = np.moveaxis(np.asarray(x, np.float32).astype(ml_dtypes.bfloat16).astype(np.float64), axis, -1)
    blocks = v.reshape(v.shape[:-1] + (-1, 32))
    amax = np.abs(blocks).max(-1, keepdims=True)
    byte = np.maximum(np.where(amax > 0, np.frexp(amax)[1] - 1 + 127, 0) - down, 1)
    scale = np.exp2(byte - 127.0)
    codes = (blocks / scale).astype(np.float32).astype(dtype).astype(np.float64)
    return np.moveaxis((codes * scale).reshape(v.shape), -1, axis)


WIDE = False


def mx_kscale(k):
    if not WIDE:
        return np.ones(k)
    levels = np.array([10, -10, 5, -5, 0])
    if k % 512:
        return np.exp2(np.random.permutation(np.resize(levels, k // 32))).repeat(32)
    a = np.empty((k // 512, 16))
    for p in range(k // 512):
        a[p, :8] = np.random.permutation(np.resize(levels, 8))
        for g in range(8):
            far = levels[np.abs(levels - a[p, g]) >= 10]
            a[p, g + 8] = far[np.random.randint(len(far))]
    return np.exp2(a.ravel()).repeat(32)


def f64(x):
    return np.asarray(x).astype(np.float64)


def striped(idx):
    return np.tile(idx.reshape(-1, 16).T, (8, 1)).astype(np.uint16)


def unstriped(offs):
    return offs[:16].T.reshape(-1).astype(np.int64)


E2M1 = np.array([0.0, 0.5, 1.0, 1.5, 2.0, 3.0, 4.0, 6.0, -0.0, -0.5, -1.0, -1.5, -2.0, -3.0, -4.0, -6.0])


def pack_weight(w, fmt):
    k, n = w.shape
    w = f64(np.asarray(w, np.float32).astype(ml_dtypes.bfloat16)).reshape(k // 32, 32, n)
    amax = np.abs(w).max(1)
    if fmt == "e4m3":
        byte = np.frexp(amax)[1] - 1 + 127 - 7
    else:
        mant, ex = np.frexp(amax / 6.0)
        byte = np.where(mant > 0.5, ex, ex - 1) + 127
    byte = np.clip(np.where(amax > 0, byte, 1), 1, 254)
    scaled = (w * np.exp2(127.0 - byte)[:, None, :]).reshape(k, n).astype(np.float32)
    by_word = np.ascontiguousarray(scaled.reshape(k // 512, 128, 4, n).transpose(0, 1, 3, 2))
    if fmt == "e4m3":
        words = by_word.astype(ml_dtypes.float8_e4m3fn).view(np.uint8)
    else:
        c = by_word.astype(ml_dtypes.float4_e2m1fn).view(np.uint8) & 0xF
        words = (c[..., 0::2] | (c[..., 1::2] << 4)).reshape(k // 512, 128, 2 * n)
    return np.ascontiguousarray(words), np.ascontiguousarray(byte.astype(np.uint8).reshape(k // 512, 16, n))


def unpack_weight(words, scales, fmt):
    g, _, n = scales.shape
    words = np.ascontiguousarray(words).reshape(g, 128, n, -1)
    if fmt == "e4m3":
        vals = words.view(ml_dtypes.float8_e4m3fn).astype(np.float64)
    else:
        nib = np.empty((g, 128, n, 4), np.uint8)
        nib[..., 0::2] = words & 0xF
        nib[..., 1::2] = words >> 4
        vals = E2M1[nib]
    vals = vals * np.repeat(np.exp2(scales.astype(np.float64) - 127.0), 8, axis=1)[..., None]
    return vals.transpose(0, 1, 3, 2).reshape(g * 512, n)


def silu(v):
    return v / (1.0 + np.exp(-np.maximum(v, -700.0)))


K, T, E, C, H, N = 512, 512, 6, 256, 512, 256
TOP = 3


def by_expert(wq, xq):
    return np.concatenate([wq[e].T @ xq[:, e * C:(e + 1) * C] for e in range(E)], axis=1)


def setup_inputs():
    n = np.random.standard_normal
    s = mx_kscale(K)[:, None]
    u = mx_kscale(H)
    deal = np.repeat(np.arange(E), C).reshape(TOP, T)[:, np.random.permutation(T)]
    deal = np.take_along_axis(deal, np.argsort(np.random.rand(TOP, T), axis=0), axis=0)
    for _ in range(8):
        s_, t_ = np.random.permutation(T).reshape(2, -1); r = np.random.randint(TOP, size=T // 2); x, y = deal[r, s_].copy(), deal[r, t_].copy()
        ok = ~((deal[:, s_] == y).any(0) | (deal[:, t_] == x).any(0)); deal[r[ok], s_[ok]] = y[ok]; deal[r[ok], t_[ok]] = x[ok]
    order = np.lexsort((np.random.rand(TOP * T), deal.reshape(-1)))
    slot_token = order % T; pos = np.empty(TOP * T, np.int64); pos[order] = np.arange(TOP * T); pos = pos.reshape(TOP, T)
    g = np.random.uniform(0.5, 1.5, (TOP, T)); g = g / g.sum(0)
    w1 = [pack_weight(m, "e2m1") for m in n((E, K, H)) / np.sqrt(K) / s[None]]
    w3 = [pack_weight(m, "e2m1") for m in n((E, K, H)) / np.sqrt(K) / s[None] * u[None, None, :]]
    w2 = [pack_weight(m, "e2m1") for m in n((E, H, N)) / np.sqrt(H) / u[None, :, None]]
    w_slot = np.empty(E * C)
    for r in range(TOP): w_slot[pos[r]] = g[r]
    return {
        "xT": (n((K, T)) * s).astype(np.float32),
        "w1_words": np.stack([m[0] for m in w1]),
        "w1_scales": np.stack([m[1] for m in w1]),
        "w3_words": np.stack([m[0] for m in w3]),
        "w3_scales": np.stack([m[1] for m in w3]),
        "w2_words": np.stack([m[0] for m in w2]),
        "w2_scales": np.stack([m[1] for m in w2]),
        "gate": np.tile(w_slot, (K, 1)).astype(np.float32),
        "offs": striped(slot_token),
        "pos1": striped(pos[0]),
        "pos2": striped(pos[1]),
        "pos3": striped(pos[2]),
    }


def reference(xT, w1_words, w1_scales, w3_words, w3_scales, w2_words, w2_scales, gate, offs, pos1, pos2, pos3):
    idx = unstriped(offs)
    w1 = np.stack([unpack_weight(w1_words[e], w1_scales[e], "e2m1") for e in range(E)])
    w3 = np.stack([unpack_weight(w3_words[e], w3_scales[e], "e2m1") for e in range(E)])
    w2 = np.stack([unpack_weight(w2_words[e], w2_scales[e], "e2m1") for e in range(E)])
    xq = mxq(f64(gate) * f64(xT)[:, idx], 0, "e4m3")
    h = silu(by_expert(w1, xq))
    h = h * by_expert(w3, xq)
    y = by_expert(w2, mxq(h, 0, "e4m3"))
    return y[:, unstriped(pos1)] + y[:, unstriped(pos2)] + y[:, unstriped(pos3)]

@@ -1,0 +1,180 @@
+from contextlib import ExitStack
+
+import concourse.mybir as mybir
+from concourse.masks import make_identity
+
+F32 = mybir.dt.float32
+BF16 = mybir.dt.bfloat16
+I32 = mybir.dt.int32
+U32 = mybir.dt.uint32
+U16 = mybir.dt.uint16
+U8 = mybir.dt.uint8
+FP8X4 = mybir.dt.float8_e4m3fn_x4
+FP4X4 = mybir.dt.float4_e2m1fn_x4
+MULT = mybir.AluOpType.mult
+ADD = mybir.AluOpType.add
+SILU = mybir.ActivationFunctionType.Silu
+
+P = 128
+K, T, E, C, H, N = 512, 512, 6, 256, 512, 256
+S = E * C
+FLOPS = 2 * S * (2 * K * H + H * N)
+BYTES = 4 * K * T + 4 * S + E * (2 * (K * H // 2 + K * H // 32) + H * N // 2 + H * N // 32) + 2 * P * (S + 3 * T) // 16 + 4 * N * T
+GATE_CUTS = (0, 256, 512, S)
+CHUNKS = [(e * C, C) for e in range(E - 1)] + [((E - 1) * C, P), ((E - 1) * C + P, P)]
+W_FIRST = 2
+
+
+def tile_moe_pre_glu_silu_kernel(tc, xT, w1_words, w1_scales, w3_words, w3_scales, w2_words, w2_scales, gate, offs, pos1, pos2, pos3, out):
+    nc = tc.nc
+    with ExitStack() as ctx:
+        keep = ctx.enter_context(tc.tile_pool(name="keep", bufs=1))
+        ring = ctx.enter_context(tc.tile_pool(name="ring", bufs=2))
+        psum = ctx.enter_context(tc.psum_pool(name="psum", bufs=2))
+
+        offs_sb = keep.tile([P, S // 16], U16, name="offs_sb")
+        pos_sb = [keep.tile([P, T // 16], U16, name="pos_sb%d" % r) for r in range(3)]
+        x_sb = [keep.tile([P, T], F32, name="x_sb%d" % j) for j in range(4)]
+        gate_sb = [keep.tile([P, GATE_CUTS[g + 1] - GATE_CUTS[g]], F32, name="gate_sb%d" % g) for g in range(3)]
+        w_a = [keep.tile([P, W_FIRST * 2 * H], U8, name="w_a%d" % m, align_bytes=64) for m in range(2)]
+        w_b = [keep.tile([P, (E - W_FIRST) * 2 * H], U8, name="w_b%d" % m, align_bytes=64) for m in range(2)]
+        w2_sb = keep.tile([P, E * 2 * N], U8, name="w2_sb", align_bytes=64)
+        sc = [keep.tile([P, E * H], U8, name="sc%d" % m, align_bytes=64) for m in range(2)]
+        sc2 = keep.tile([P, E * N], U8, name="sc2", align_bytes=64)
+        ident = keep.tile([P, P], F32, name="ident")
+        y_sb = [keep.tile([P, S], F32, name="y_sb%d" % b) for b in range(2)]
+        warm_in = keep.tile([P, 1], F32, name="warm_in")
+        warm_out = keep.tile([P, 1], F32, name="warm_out")
+
+        nc.vector.memset(sc[0][:].bitcast(I32), 0)
+        nc.gpsimd.memset(sc[1][:].bitcast(I32), 0)
+        nc.vector.memset(sc2[:].bitcast(I32), 0)
+        nc.vector.memset(warm_in[:], 0.0)
+        nc.scalar.activation(warm_out[:], warm_in[:], SILU)
+        make_identity(nc, ident[:])
+
+        def load_words(dst, words, e0, e1):
+            src = words[e0:e1, 0].rearrange("e p b -> p e b").bitcast(I32)
+            nc.sync.dma_start(dst[:].bitcast(I32).rearrange("p (e b) -> p e b", e=e1 - e0), src)
+
+        def load_scales(dst, scales):
+            src = scales[:, 0].rearrange("e (q r) i -> r q e i", r=4)
+            for r in range(4):
+                nc.sync.dma_start(dst[r:P:32, :].bitcast(I32).rearrange("q (e i) -> q e i", e=E), src[r].bitcast(I32))
+
+        def load_gate(g, queue):
+            queue.dma_start(gate_sb[g][:], gate[0:P, GATE_CUTS[g]:GATE_CUTS[g + 1]])
+
+        x_rows = xT.rearrange("(p j) t -> j p t", j=4)
+        nc.sync.dma_start(x_sb[0][:], x_rows[0])
+        nc.sync.dma_start(offs_sb[:], offs)
+        load_gate(0, nc.sync)
+        for j in range(1, 4):
+            nc.sync.dma_start(x_sb[j][:], x_rows[j])
+        load_gate(1, nc.sync)
+        load_gate(2, nc.sync)
+        load_scales(sc[0], w1_scales)
+        load_scales(sc[1], w3_scales)
+        load_words(w_a[0], w1_words, 0, W_FIRST)
+        load_words(w_a[1], w3_words, 0, W_FIRST)
+        load_scales(sc2, w2_scales)
+        load_words(w_b[0], w1_words, W_FIRST, E)
+        load_words(w_b[1], w3_words, W_FIRST, E)
+        load_words(w2_sb, w2_words, 0, E)
+        for r, pos in enumerate((pos1, pos2, pos3)):
+            nc.sync.dma_start(pos_sb[r][:], pos)
+
+        def gate_of(s0, n):
+            g = max(i for i in range(3) if GATE_CUTS[i] <= s0)
+            return gate_sb[g][:, s0 - GATE_CUTS[g]:s0 - GATE_CUTS[g] + n]
+
+        def w_of(m, e):
+            if e < W_FIRST:
+                return w_a[m][:, e * 2 * H:(e + 1) * 2 * H]
+            return w_b[m][:, (e - W_FIRST) * 2 * H:(e - W_FIRST + 1) * 2 * H]
+
+        xg, xb, xq, bank_b, sil, ht, hb, hq, bank_y = {}, {}, {}, {}, {}, {}, {}, {}, {}
+
+        def gather(c):
+            s0, n = CHUNKS[c]
+            xg[c] = ring.tile([P, 4, n], F32, name="xg")
+            lst = offs_sb[:, s0 // 16:(s0 + n) // 16]
+            for j in range(4):
+                nc.vector.tensor_tensor(xg[c][:, j, :], x_sb[j][:].indirect(lst), gate_of(s0, n), MULT)
+
+        def weave(c):
+            n = CHUNKS[c][1]
+            xb[c] = ring.tile([P, 4 * n], BF16, name="xb", align_bytes=64)
+            nc.scalar.copy(xb[c][:].rearrange("p (c i j) -> p c j i", i=4, j=4), xg[c][:].rearrange("p j (c i) -> p c j i", i=4))
+
+        def quant(src, n, name):
+            codes = ring.tile([P, n], U32, name=name + "_codes", align_bytes=64)
+            scales = ring.tile([P, n], U8, name=name + "_scales", align_bytes=64)
+            nc.vector.quantize_mx(out=codes[:].bitcast(FP8X4), scales=scales[:], in_=src[:])
+            return codes, scales
+
+        def layer1(c):
+            s0, n = CHUNKS[c]
+            e = s0 // C
+            codes, scales = quant(xb[c], n, "xq")
+            for t in range(n // P):
+                cols = slice(t * P, (t + 1) * P)
+                banks = [psum.tile([P, H], F32, name="bank_a"), psum.tile([P, H], F32, name="bank_b")]
+                for m in range(2):
+                    nc.tensor.matmul_mx(out=banks[m][:], lhsT=codes[:, cols].bitcast(FP8X4), lhsT_scale=scales[:, cols],
+                                        rhs=w_of(m, e).bitcast(FP4X4), rhs_scale=sc[m][:, e * H:(e + 1) * H], start=True, stop=True)
+                bank_b[c, t] = banks[1]
+                sil[c, t] = ring.tile([P, H], F32, name="sil", bufs=4)
+                nc.scalar.activation(sil[c, t][:].rearrange("s (u p d) -> s u p d", u=2, d=2),
+                                     banks[0][:].rearrange("s (p u d) -> s u p d", u=2, d=2), SILU)
+
+        def product(c):
+            n = CHUNKS[c][1]
+            ht[c] = psum.tile([P, 2, n], F32, name="bank_t")
+            for t in range(n // P):
+                h = ring.tile([P, H], BF16, name="h", bufs=3, align_bytes=64)
+                nc.vector.tensor_tensor(h[:].rearrange("s (u p d) -> s u p d", u=2, d=2),
+                                        bank_b[c, t][:].rearrange("s (p u d) -> s u p d", u=2, d=2),
+                                        sil[c, t][:].rearrange("s (u p d) -> s u p d", u=2, d=2), MULT)
+                words = h[:].bitcast(F32)
+                for u in range(2):
+                    nc.tensor.transpose(ht[c][:, u, t * P:(t + 1) * P], words[:, u * P:(u + 1) * P], ident[:])
+            hb[c] = ring.tile([P, 4 * n], BF16, name="hb", align_bytes=64)
+            nc.scalar.copy(hb[c][:].bitcast(F32).rearrange("p (s u) -> p s u", u=2), ht[c][:].rearrange("p u s -> p s u"))
+
+        def layer2(c):
+            s0, n = CHUNKS[c]
+            e = s0 // C
+            codes, scales = quant(hb[c], n, "hq")
+            if s0 % C == 0:
+                bank_y[e] = psum.tile([P, 2, C], F32, name="bank_y")
+            for b in range(2):
+                c0 = e * N + b * P
+                nc.tensor.matmul_mx(out=bank_y[e][:, b, s0 % C:s0 % C + n], lhsT=w2_sb[:, 2 * c0:2 * (c0 + P)].bitcast(FP4X4), lhsT_scale=sc2[:, c0:c0 + P],
+                                    rhs=codes[:].bitcast(FP8X4), rhs_scale=scales[:], start=True, stop=True)
+            if (s0 + n) % C == 0:
+                for b in range(2):
+                    nc.scalar.copy(y_sb[b][:, e * C:(e + 1) * C], bank_y[e][:, b, :])
+
+        count = len(CHUNKS)
+        for step in range(count + 4):
+            if step < count:
+                gather(step)
+                weave(step)
+            if 0 <= step - 1 < count:
+                layer1(step - 1)
+            if 0 <= step - 3 < count:
+                product(step - 3)
+            if 0 <= step - 4 < count:
+                layer2(step - 4)
+
+        first = [keep.tile([P, T], F32, name="first%d" % b) for b in range(2)]
+        second = [keep.tile([P, T], F32, name="second%d" % b) for b in range(2)]
+        for b in range(2):
+            nc.vector.tensor_copy(first[b][:], y_sb[b][:].indirect(pos_sb[0][:]))
+        for b in range(2):
+            nc.vector.tensor_tensor(second[b][:], y_sb[b][:].indirect(pos_sb[1][:]), first[b][:], ADD)
+        for b, t0, n in ((0, 0, T), (1, 0, T // 2), (1, T // 2, T // 2)):
+            total = keep.tile([P, n], F32, name="total%d_%d" % (b, t0))
+            nc.vector.tensor_tensor(total[:], y_sb[b][:].indirect(pos_sb[2][:, t0 // 16:(t0 + n) // 16]), second[b][:, t0:t0 + n], ADD)
+            nc.sync.dma_start(out[b * P:(b + 1) * P, t0:t0 + n], total[:])

@@ -104,11 +104,10 @@ def tile_moe_pre_glu_silu_kernel(tc, xT, w1_words, w1_scales, w3_words, w3_scale
 
         def weave(c):
             n = CHUNKS[c][1]
-            xb[c] = ring.tile([P, 4 * n], BF16, name="xb", align_bytes=64)
+            xb[c] = keep.tile([P, 4 * n], BF16, name="xb", tag="turn%d" % (c % 3), align_bytes=64)
             nc.scalar.copy(xb[c][:].rearrange("p (c i j) -> p c j i", i=4, j=4), xg[c][:].rearrange("p j (c i) -> p c j i", i=4))
 
-        def quant(src, n, name):
-            codes = ring.tile([P, n], U32, name=name + "_codes", align_bytes=64)
+        def quant(src, n, name, codes):
             scales = ring.tile([P, n], U8, name=name + "_scales", align_bytes=64)
             nc.vector.quantize_mx(out=codes[:].bitcast(FP8X4), scales=scales[:], in_=src[:])
             return codes, scales
@@ -116,7 +115,7 @@ def tile_moe_pre_glu_silu_kernel(tc, xT, w1_words, w1_scales, w3_words, w3_scale
         def layer1(c):
             s0, n = CHUNKS[c]
             e = s0 // C
-            codes, scales = quant(xb[c], n, "xq")
+            codes, scales = quant(xb[c], n, "xq", keep.tile([P, n], U32, name="xq_codes", tag="turn%d" % ((c + 2) % 3), align_bytes=64))
             for t in range(n // P):
                 cols = slice(t * P, (t + 1) * P)
                 banks = [psum.tile([P, H], F32, name="bank_a"), psum.tile([P, H], F32, name="bank_b")]
@@ -139,13 +138,16 @@ def tile_moe_pre_glu_silu_kernel(tc, xT, w1_words, w1_scales, w3_words, w3_scale
                 words = h[:].bitcast(F32)
                 for u in range(2):
                     nc.tensor.transpose(ht[c][:, u, t * P:(t + 1) * P], words[:, u * P:(u + 1) * P], ident[:])
+
+        def turn(c):
+            n = CHUNKS[c][1]
             hb[c] = ring.tile([P, 4 * n], BF16, name="hb", align_bytes=64)
             nc.scalar.copy(hb[c][:].bitcast(F32).rearrange("p (s u) -> p s u", u=2), ht[c][:].rearrange("p u s -> p s u"))
 
         def layer2(c):
             s0, n = CHUNKS[c]
             e = s0 // C
-            codes, scales = quant(hb[c], n, "hq")
+            codes, scales = quant(hb[c], n, "hq", ring.tile([P, n], U32, name="hq_codes", align_bytes=64))
             if s0 % C == 0:
                 bank_y[e] = psum.tile([P, 2, C], F32, name="bank_y")
             for b in range(2):
@@ -163,8 +165,10 @@ def tile_moe_pre_glu_silu_kernel(tc, xT, w1_words, w1_scales, w3_words, w3_scale
                 weave(step)
             if 0 <= step - 1 < count:
                 layer1(step - 1)
+            if 0 <= step - 2 < count:
+                product(step - 2)
             if 0 <= step - 3 < count:
-                product(step - 3)
+                turn(step - 3)
             if 0 <= step - 4 < count:
                 layer2(step - 4)
 
@@ -174,7 +178,7 @@ def tile_moe_pre_glu_silu_kernel(tc, xT, w1_words, w1_scales, w3_words, w3_scale
             nc.vector.tensor_copy(first[b][:], y_sb[b][:].indirect(pos_sb[0][:]))
         for b in range(2):
             nc.vector.tensor_tensor(second[b][:], y_sb[b][:].indirect(pos_sb[1][:]), first[b][:], ADD)
-        for b, t0, n in ((0, 0, T), (1, 0, T // 2), (1, T // 2, T // 2)):
+        for b, t0, n in ((0, 0, T), (1, 0, T - P), (1, T - P, P)):
             total = keep.tile([P, n], F32, name="total%d_%d" % (b, t0))
             nc.vector.tensor_tensor(total[:], y_sb[b][:].indirect(pos_sb[2][:, t0 // 16:(t0 + n) // 16]), second[b][:, t0:t0 + n], ADD)
-            nc.sync.dma_start(out[b * P:(b + 1) * P, t0:t0 + n], total[:])
+            (nc.scalar if t0 else nc.sync).dma_start(out[b * P:(b + 1) * P, t0:t0 + n], total[:])

@@ -20,9 +20,9 @@ K, T, E, C, H, N = 512, 512, 6, 256, 512, 256
 S = E * C
 FLOPS = 2 * S * (2 * K * H + H * N)
 BYTES = 4 * K * T + 4 * S + E * (2 * (K * H // 2 + K * H // 32) + H * N // 2 + H * N // 32) + 2 * P * (S + 3 * T) // 16 + 4 * N * T
-GATE_CUTS = (0, 256, 512, S)
+GATE_CUTS = (0, 256, 768, S)
 CHUNKS = [(e * C, C) for e in range(E - 1)] + [((E - 1) * C, P), ((E - 1) * C + P, P)]
-W_FIRST = 2
+W_CUTS = (0, 1, 3, E)
 
 
 def tile_moe_pre_glu_silu_kernel(tc, xT, w1_words, w1_scales, w3_words, w3_scales, w2_words, w2_scales, gate, offs, pos1, pos2, pos3, out):
@@ -36,8 +36,7 @@ def tile_moe_pre_glu_silu_kernel(tc, xT, w1_words, w1_scales, w3_words, w3_scale
         pos_sb = [keep.tile([P, T // 16], U16, name="pos_sb%d" % r) for r in range(3)]
         x_sb = [keep.tile([P, T], F32, name="x_sb%d" % j) for j in range(4)]
         gate_sb = [keep.tile([P, GATE_CUTS[g + 1] - GATE_CUTS[g]], F32, name="gate_sb%d" % g) for g in range(3)]
-        w_a = [keep.tile([P, W_FIRST * 2 * H], U8, name="w_a%d" % m, align_bytes=64) for m in range(2)]
-        w_b = [keep.tile([P, (E - W_FIRST) * 2 * H], U8, name="w_b%d" % m, align_bytes=64) for m in range(2)]
+        w_sb = [[keep.tile([P, (W_CUTS[g + 1] - W_CUTS[g]) * 2 * H], U8, name="w_sb%d_%d" % (m, g), align_bytes=64) for g in range(3)] for m in range(2)]
         w2_sb = keep.tile([P, E * 2 * N], U8, name="w2_sb", align_bytes=64)
         sc = [keep.tile([P, E * H], U8, name="sc%d" % m, align_bytes=64) for m in range(2)]
         sc2 = keep.tile([P, E * N], U8, name="sc2", align_bytes=64)
@@ -72,14 +71,14 @@ def tile_moe_pre_glu_silu_kernel(tc, xT, w1_words, w1_scales, w3_words, w3_scale
         for j in range(1, 4):
             nc.sync.dma_start(x_sb[j][:], x_rows[j])
         load_gate(1, nc.sync)
-        load_gate(2, nc.sync)
         load_scales(sc[0], w1_scales)
         load_scales(sc[1], w3_scales)
-        load_words(w_a[0], w1_words, 0, W_FIRST)
-        load_words(w_a[1], w3_words, 0, W_FIRST)
+        for g in range(3):
+            load_words(w_sb[0][g], w1_words, W_CUTS[g], W_CUTS[g + 1])
+            load_words(w_sb[1][g], w3_words, W_CUTS[g], W_CUTS[g + 1])
+            if g == 0:
+                load_gate(2, nc.sync)
         load_scales(sc2, w2_scales)
-        load_words(w_b[0], w1_words, W_FIRST, E)
-        load_words(w_b[1], w3_words, W_FIRST, E)
         load_words(w2_sb, w2_words, 0, E)
         for r, pos in enumerate((pos1, pos2, pos3)):
             nc.sync.dma_start(pos_sb[r][:], pos)
@@ -89,9 +88,8 @@ def tile_moe_pre_glu_silu_kernel(tc, xT, w1_words, w1_scales, w3_words, w3_scale
             return gate_sb[g][:, s0 - GATE_CUTS[g]:s0 - GATE_CUTS[g] + n]
 
         def w_of(m, e):
-            if e < W_FIRST:
-                return w_a[m][:, e * 2 * H:(e + 1) * 2 * H]
-            return w_b[m][:, (e - W_FIRST) * 2 * H:(e - W_FIRST + 1) * 2 * H]
+            g = max(i for i in range(3) if W_CUTS[i] <= e)
+            return w_sb[m][g][:, (e - W_CUTS[g]) * 2 * H:(e - W_CUTS[g] + 1) * 2 * H]
 
         xg, xb, xq, bank_b, sil, ht, hb, hq, bank_y = {}, {}, {}, {}, {}, {}, {}, {}, {}
 

from contextlib import ExitStack

import concourse.mybir as mybir
from concourse.masks import make_identity

F32 = mybir.dt.float32
BF16 = mybir.dt.bfloat16
I32 = mybir.dt.int32
U32 = mybir.dt.uint32
U16 = mybir.dt.uint16
U8 = mybir.dt.uint8
FP8X4 = mybir.dt.float8_e4m3fn_x4
FP4X4 = mybir.dt.float4_e2m1fn_x4
MULT = mybir.AluOpType.mult
ADD = mybir.AluOpType.add
SILU = mybir.ActivationFunctionType.Silu

P = 128
K, T, E, C, H, N = 512, 512, 6, 256, 512, 256
S = E * C
FLOPS = 2 * S * (2 * K * H + H * N)
BYTES = 4 * K * T + 4 * S + E * (2 * (K * H // 2 + K * H // 32) + H * N // 2 + H * N // 32) + 2 * P * (S + 3 * T) // 16 + 4 * N * T
GATE_CUTS = (0, 256, 768, S)
CHUNKS = [(e * C, C) for e in range(E - 1)] + [((E - 1) * C, P), ((E - 1) * C + P, P)]
W_CUTS = (0, 1, 3, E)


def tile_moe_pre_glu_silu_kernel(tc, xT, w1_words, w1_scales, w3_words, w3_scales, w2_words, w2_scales, gate, offs, pos1, pos2, pos3, out):
    nc = tc.nc
    with ExitStack() as ctx:
        keep = ctx.enter_context(tc.tile_pool(name="keep", bufs=1))
        ring = ctx.enter_context(tc.tile_pool(name="ring", bufs=2))
        psum = ctx.enter_context(tc.psum_pool(name="psum", bufs=2))

        offs_sb = keep.tile([P, S // 16], U16, name="offs_sb")
        pos_sb = [keep.tile([P, T // 16], U16, name="pos_sb%d" % r) for r in range(3)]
        x_sb = [keep.tile([P, T], F32, name="x_sb%d" % j) for j in range(4)]
        gate_sb = [keep.tile([P, GATE_CUTS[g + 1] - GATE_CUTS[g]], F32, name="gate_sb%d" % g) for g in range(3)]
        w_sb = [[keep.tile([P, (W_CUTS[g + 1] - W_CUTS[g]) * 2 * H], U8, name="w_sb%d_%d" % (m, g), align_bytes=64) for g in range(3)] for m in range(2)]
        w2_sb = keep.tile([P, E * 2 * N], U8, name="w2_sb", align_bytes=64)
        sc = [keep.tile([P, E * H], U8, name="sc%d" % m, align_bytes=64) for m in range(2)]
        sc2 = keep.tile([P, E * N], U8, name="sc2", align_bytes=64)
        ident = keep.tile([P, P], F32, name="ident")
        y_sb = [keep.tile([P, S], F32, name="y_sb%d" % b) for b in range(2)]
        warm_in = keep.tile([P, 1], F32, name="warm_in")
        warm_out = keep.tile([P, 1], F32, name="warm_out")

        nc.vector.memset(sc[0][:].bitcast(I32), 0)
        nc.gpsimd.memset(sc[1][:].bitcast(I32), 0)
        nc.vector.memset(sc2[:].bitcast(I32), 0)
        nc.vector.memset(warm_in[:], 0.0)
        nc.scalar.activation(warm_out[:], warm_in[:], SILU)
        make_identity(nc, ident[:])

        def load_words(dst, words, e0, e1):
            src = words[e0:e1, 0].rearrange("e p b -> p e b").bitcast(I32)
            nc.sync.dma_start(dst[:].bitcast(I32).rearrange("p (e b) -> p e b", e=e1 - e0), src)

        def load_scales(dst, scales):
            src = scales[:, 0].rearrange("e (q r) i -> r q e i", r=4)
            for r in range(4):
                nc.sync.dma_start(dst[r:P:32, :].bitcast(I32).rearrange("q (e i) -> q e i", e=E), src[r].bitcast(I32))

        def load_gate(g, queue):
            queue.dma_start(gate_sb[g][:], gate[0:P, GATE_CUTS[g]:GATE_CUTS[g + 1]])

        x_rows = xT.rearrange("(p j) t -> j p t", j=4)
        nc.sync.dma_start(x_sb[0][:], x_rows[0])
        nc.sync.dma_start(offs_sb[:], offs)
        load_gate(0, nc.sync)
        for j in range(1, 4):
            nc.sync.dma_start(x_sb[j][:], x_rows[j])
        load_gate(1, nc.sync)
        load_scales(sc[0], w1_scales)
        load_scales(sc[1], w3_scales)
        for g in range(3):
            load_words(w_sb[0][g], w1_words, W_CUTS[g], W_CUTS[g + 1])
            load_words(w_sb[1][g], w3_words, W_CUTS[g], W_CUTS[g + 1])
            if g == 0:
                load_gate(2, nc.sync)
        load_scales(sc2, w2_scales)
        load_words(w2_sb, w2_words, 0, E)
        for r, pos in enumerate((pos1, pos2, pos3)):
            nc.sync.dma_start(pos_sb[r][:], pos)

        def gate_of(s0, n):
            g = max(i for i in range(3) if GATE_CUTS[i] <= s0)
            return gate_sb[g][:, s0 - GATE_CUTS[g]:s0 - GATE_CUTS[g] + n]

        def w_of(m, e):
            g = max(i for i in range(3) if W_CUTS[i] <= e)
            return w_sb[m][g][:, (e - W_CUTS[g]) * 2 * H:(e - W_CUTS[g] + 1) * 2 * H]

        xg, xb, xq, bank_b, sil, ht, hb, hq, bank_y = {}, {}, {}, {}, {}, {}, {}, {}, {}

        def gather(c):
            s0, n = CHUNKS[c]
            xg[c] = ring.tile([P, 4, n], F32, name="xg")
            lst = offs_sb[:, s0 // 16:(s0 + n) // 16]
            for j in range(4):
                nc.vector.tensor_tensor(xg[c][:, j, :], x_sb[j][:].indirect(lst), gate_of(s0, n), MULT)

        def weave(c):
            n = CHUNKS[c][1]
            xb[c] = keep.tile([P, 4 * n], BF16, name="xb", tag="turn%d" % (c % 3), align_bytes=64)
            nc.scalar.copy(xb[c][:].rearrange("p (c i j) -> p c j i", i=4, j=4), xg[c][:].rearrange("p j (c i) -> p c j i", i=4))

        def quant(src, n, name, codes):
            scales = ring.tile([P, n], U8, name=name + "_scales", align_bytes=64)
            nc.vector.quantize_mx(out=codes[:].bitcast(FP8X4), scales=scales[:], in_=src[:])
            return codes, scales

        def layer1(c):
            s0, n = CHUNKS[c]
            e = s0 // C
            codes, scales = quant(xb[c], n, "xq", keep.tile([P, n], U32, name="xq_codes", tag="turn%d" % ((c + 2) % 3), align_bytes=64))
            for t in range(n // P):
                cols = slice(t * P, (t + 1) * P)
                banks = [psum.tile([P, H], F32, name="bank_a"), psum.tile([P, H], F32, name="bank_b")]
                for m in range(2):
                    nc.tensor.matmul_mx(out=banks[m][:], lhsT=codes[:, cols].bitcast(FP8X4), lhsT_scale=scales[:, cols],
                                        rhs=w_of(m, e).bitcast(FP4X4), rhs_scale=sc[m][:, e * H:(e + 1) * H], start=True, stop=True)
                bank_b[c, t] = banks[1]
                sil[c, t] = ring.tile([P, H], F32, name="sil", bufs=4)
                nc.scalar.activation(sil[c, t][:].rearrange("s (u p d) -> s u p d", u=2, d=2),
                                     banks[0][:].rearrange("s (p u d) -> s u p d", u=2, d=2), SILU)

        def product(c):
            n = CHUNKS[c][1]
            ht[c] = psum.tile([P, 2, n], F32, name="bank_t")
            for t in range(n // P):
                h = ring.tile([P, H], BF16, name="h", bufs=3, align_bytes=64)
                nc.vector.tensor_tensor(h[:].rearrange("s (u p d) -> s u p d", u=2, d=2),
                                        bank_b[c, t][:].rearrange("s (p u d) -> s u p d", u=2, d=2),
                                        sil[c, t][:].rearrange("s (u p d) -> s u p d", u=2, d=2), MULT)
                words = h[:].bitcast(F32)
                for u in range(2):
                    nc.tensor.transpose(ht[c][:, u, t * P:(t + 1) * P], words[:, u * P:(u + 1) * P], ident[:])

        def turn(c):
            n = CHUNKS[c][1]
            hb[c] = ring.tile([P, 4 * n], BF16, name="hb", align_bytes=64)
            nc.scalar.copy(hb[c][:].bitcast(F32).rearrange("p (s u) -> p s u", u=2), ht[c][:].rearrange("p u s -> p s u"))

        def layer2(c):
            s0, n = CHUNKS[c]
            e = s0 // C
            codes, scales = quant(hb[c], n, "hq", ring.tile([P, n], U32, name="hq_codes", align_bytes=64))
            if s0 % C == 0:
                bank_y[e] = psum.tile([P, 2, C], F32, name="bank_y")
            for b in range(2):
                c0 = e * N + b * P
                nc.tensor.matmul_mx(out=bank_y[e][:, b, s0 % C:s0 % C + n], lhsT=w2_sb[:, 2 * c0:2 * (c0 + P)].bitcast(FP4X4), lhsT_scale=sc2[:, c0:c0 + P],
                                    rhs=codes[:].bitcast(FP8X4), rhs_scale=scales[:], start=True, stop=True)
            if (s0 + n) % C == 0:
                for b in range(2):
                    nc.scalar.copy(y_sb[b][:, e * C:(e + 1) * C], bank_y[e][:, b, :])

        count = len(CHUNKS)
        for step in range(count + 4):
            if step < count:
                gather(step)
                weave(step)
            if 0 <= step - 1 < count:
                layer1(step - 1)
            if 0 <= step - 2 < count:
                product(step - 2)
            if 0 <= step - 3 < count:
                turn(step - 3)
            if 0 <= step - 4 < count:
                layer2(step - 4)

        first = [keep.tile([P, T], F32, name="first%d" % b) for b in range(2)]
        second = [keep.tile([P, T], F32, name="second%d" % b) for b in range(2)]
        for b in range(2):
            nc.vector.tensor_copy(first[b][:], y_sb[b][:].indirect(pos_sb[0][:]))
        for b in range(2):
            nc.vector.tensor_tensor(second[b][:], y_sb[b][:].indirect(pos_sb[1][:]), first[b][:], ADD)
        for b, t0, n in ((0, 0, T), (1, 0, T - P), (1, T - P, P)):
            total = keep.tile([P, n], F32, name="total%d_%d" % (b, t0))
            nc.vector.tensor_tensor(total[:], y_sb[b][:].indirect(pos_sb[2][:, t0 // 16:(t0 + n) // 16]), second[b][:, t0:t0 + n], ADD)
            (nc.scalar if t0 else nc.sync).dma_start(out[b * P:(b + 1) * P, t0:t0 + n], total[:])
